import numpy as np, ml_dtypes
CORES = [2,6,10,14,18,22,26,30]
N = 8
import mx_ref
BF = ml_dtypes.bfloat16
def gentries(a):
    return np.ascontiguousarray(a.reshape(8, 16, -1).transpose(0, 2, 1)).reshape(8, -1)
def gtable(e):
    e = np.asarray(e); return np.ascontiguousarray(e.reshape(8, -1, 16).transpose(0, 2, 1)).reshape(128, -1).astype(np.int32)
def gcols(t, e):
    v = np.concatenate([t.reshape(8, 16, -1, 4), np.zeros((8, 16, 1, 4), BF)], axis=2)
    return np.ascontiguousarray(np.stack([v[g][:, e[g]] for g in range(8)])).reshape(128, -1)
def cols(t, e):
    v = np.concatenate([t.reshape(128, -1, 4), np.zeros((128, 1, 4), BF)], axis=1)
    return np.ascontiguousarray(v[:, e]).reshape(128, -1)
def tile(rs):
    return np.stack(rs, axis=2).reshape(128, -1).astype(BF)
def pick(q, e):
    c = np.concatenate([q[0].reshape(128, -1, 4), np.zeros((128, 1, 4), np.uint8)], axis=1); s = np.concatenate([q[1], np.ones((16, 1), np.uint8)], axis=1)
    return (np.ascontiguousarray(c[:, e].reshape(128, -1)), np.ascontiguousarray(s[:, e]))
def join(*qs):
    return (np.concatenate([q[0] for q in qs], axis=1), np.concatenate([q[1] for q in qs], axis=1))
def put(q, e, v):
    c, s = q[0].reshape(128, -1, 4).copy(), q[1].copy(); c[:, e] = v[0].reshape(128, -1, 4); s[:, e] = v[1]
    return (c.reshape(128, -1), s)
def pk(c, s):
    return (np.ascontiguousarray(c), mx_ref.live(s))
def emit(q):
    return q[0], q[1]
def packed(v, rng):
    q = [mx_ref.quantize(np.ascontiguousarray(v[r])) for r in range(N)]
    return np.stack([a for a, b in q]), np.stack([mx_ref.plane(b, rng) for a, b in q])
def values_of_codes():
    e, c = np.zeros((128, 128, 4), np.float32), np.zeros((128, 2, 4), np.uint8)
    e[np.arange(128), np.arange(128), 0] = 1
    c[:127, :, 0] = np.arange(256).reshape(2, 128).T[:127]
    return mx_ref.matmul(mx_ref.quantize(e.reshape(128, 512).astype(BF)), (c.reshape(128, 8), np.full((16, 2), 127, np.uint8))).T.reshape(-1).astype(np.float64)
CODE_VALUE, SCALE_VALUE = values_of_codes(), 2.0 ** (np.arange(256) - 127.0)
def decode(q):
    return (CODE_VALUE[q[0]].reshape(16, 8, -1, 4) * SCALE_VALUE[q[1]][:, None, :, None] + 0.0).reshape(128, -1).astype(np.float32)
def f(rng, *shape):
    return mx_ref.flush((rng.standard_normal(shape, dtype=np.float32) * np.exp2(rng.integers(-2, 3, shape[:-1] + (1,)))).astype(BF))
def wide(rng, *shape, cols=0):
    v = rng.standard_normal(shape, dtype=np.float32) * np.exp2(rng.integers(-12, 13, shape)).astype(np.float32)
    if cols: v *= np.repeat(np.exp2(rng.integers(-cols, cols + 1, shape[:-2] + (1, shape[-1] // 4))) * (rng.random(shape[:-2] + (1, shape[-1] // 4)) > 0.0625), 4, axis=-1).astype(np.float32)
    return mx_ref.flush(v.astype(BF))
C, J, K, R = 320, 512, 128, 3
def big(v):
    v = v.astype(np.float32)
    v[np.abs(v) < np.float32(2.0 ** -16)] = 0
    return v.astype(BF)
def numbers_of(rng):
    return {"x": big(f(rng, N, 128, 4 * C)), "u": np.array(f(rng, N, 128, 512)), "v": np.array(f(rng, N, 128, 512))}
def paths(rng, n):
    a = np.zeros((8, J), np.int64)
    a[0] = rng.integers(0, C, J)
    for g in range(1, 8):
        a[g] = np.where(rng.random(J) < 0.5, a[g - 1], n[rng.integers(0, 8, J), a[g - 1]])
    return a
def lists(rng):
    n = rng.integers(0, C, (8, C))
    return {"nb": np.stack([gtable(n)] * N), "p": np.stack([gtable(paths(rng, n)) for r in range(N)])}
def weights(rng, kept=[]):
    w = (rng.random((N, 128, 512, 4), dtype=np.float32) * 2 - 1) * np.float32(2.0 ** -6)
    for i in range(2):
        k = rng.integers(0, 512, (N, 512))
        w[np.arange(N)[:, None], k >> 2, np.arange(512)[None], k & 3] = (3 + 6 * rng.random((N, 512))) * rng.choice([-1.0, 1.0], (N, 512))
    w = w.reshape(N, 128, 4, 128, 4)
    for i in kept:
        for h in range(i, 128, 16):
            w[:, :, :, h] = 0
            for b in range(4): w[:, h, b, h, b] = 32
    c, s = packed(w.reshape(N, 128, 2048).astype(BF), rng)
    return {"wc": c, "ws": s}
def setup_inputs(rng):
    return {**numbers_of(rng), **lists(rng), **weights(rng)}
def setup_inputs_ties(rng):
    d = numbers_of(rng)
    x = d["x"].reshape(N, 8, 16, C, 4)
    k = rng.integers(0, 3, (N, 8, C))
    k[:, rng.permutation(8)[:3]] = 1
    x[:, :, 0] = 0
    x[:, :, 0, :, 0] = k.astype(np.float32).astype(BF)
    z = (N, 8, 8, C, 4)
    odd = (1 + (2 * rng.integers(0, 64, z) + 1) * 2.0 ** -7) * np.exp2(-1.0 * rng.integers(8, 15, z)) * rng.choice([-1.0, 1.0], z)
    odd[:, :, 0, :, 0] = 1.96875
    o = rng.permutation(N)
    odd[o[2], :, 0, :, 1] = rng.integers(2, 32, (8, C)) * 2.0 ** -17
    x[:, :, 8:] = odd.astype(np.float32).astype(BF)
    u = d["u"].reshape(N, 128, 128, 4)
    u[:, :, ::16] = 0
    for r in range(N):
        for h in range(0, 128, 16):
            if r == o[2]: u[r, h + 8, h, 1] = 1.0
            else: u[r, h, h, 0] = 0.0 if r == o[0] else -1.0 if r == o[1] else 1.0
    l = lists(rng)
    t = np.array(gentries(l["p"][o[0]]))
    t[:, rng.permutation(J)[:J // 4]] = C - 32 + 4 * rng.integers(0, 8, (1, J // 4)) + np.arange(8)[:, None] % 2
    l["p"][o[0]] = gtable(t)
    return {"x": x.reshape(N, 128, 4 * C), "u": u.reshape(N, 128, 512), "v": d["v"], **l, **weights(rng, [0])}
def setup_inputs_near(rng):
    d = numbers_of(rng)
    x = d["x"].astype(np.float32).reshape(N, 8, 16, C, 4)
    x[:, :, :2] = 0
    x[:, :, 2:8] *= np.float32(0.25)
    x[:, :, 8:] = 0
    x[:, :, 0, :, 0] = 1
    x[:, :, 1, :, 0] = 2.0 ** -10
    s = rng.integers(0, 16, (N, 8, C))
    x[:, :, 8] = ((s[:, :, :, None] >> np.arange(4)) & 1) * np.exp2(np.arange(4) - 24.0)
    x[:, :, 10, :, 0] = (1 + 0.125 * rng.integers(0, 8, (N, 8, C))) * 2.0 ** -30
    x[:, :, 12] = x[:, :, 10]
    u = d["u"].reshape(N, 128, 128, 4)
    u[:, :, ::16] = 0
    o = rng.permutation(N) % 4
    for r in range(N):
        k = 2.0 ** -30 if o[r] in (1, 3) else 1.0
        sign = rng.permutation(8) % 2 * 2.0 - 1.0
        for g in range(8):
            h = 16 * g
            if o[r] == 3:
                u[r, h + 10, h, 0] = 1.125 * k * sign[g]
                u[r, h + 12, h, 0] = -k * sign[g]
            else:
                u[r, h, h, 0] = -k if o[r] == 2 else k
                u[r, h + 1, h, 0] = k
                u[r, h + 8, h] = 2 * k
    return {"x": x.reshape(N, 128, 4 * C).astype(BF), "u": u.reshape(N, 128, 512), "v": d["v"], **lists(rng), **weights(rng, [0, 1, 8, 9, 10, 11, 12, 13, 14, 15])}
def setup_inputs_huge(rng):
    d = numbers_of(rng)
    h = rng.permutation(8)
    x = -0.95 - 0.05 * rng.random((N, 8, 16, C, 4))
    x[:, h[4:]] = (0.75 + 0.1 * rng.random((N, 4, 16, C, 4))) * rng.choice([-1.0, 1.0], (N, 4, 1, C, 1))
    u = d["u"].reshape(N, 128, 128, 4)
    u[:, :, ::16] = 0
    for r in range(N):
        below = rng.permutation(8) < 4
        for g in range(8):
            a = 16 * int(rng.choice(h[:4] if below[g] else h[4:]))
            u[r, a:a + 16, 16 * g] = (2.0 ** 30 * (1 - 0.1 * rng.random((16, 4)))).astype(np.float32).astype(BF)
    return {"x": (2.0 ** 30 * x).astype(np.float32).reshape(N, 128, 4 * C).astype(BF), "u": u.reshape(N, 128, 512), "v": d["v"], **lists(rng), **weights(rng)}
def setup_inputs_ends(rng):
    d = numbers_of(rng)
    o = rng.permutation(N)
    sign = rng.integers(0, 2, (8, 16, 1, 4)) * 2.0 - 1.0
    x = np.zeros((N, 8, 16, C, 4))
    u = d["u"].reshape(N, 128, 128, 4)
    u[:, :, ::16] = 0
    v = np.zeros((N, 128, 512))
    n = rng.integers(0, C, (8, C))
    j = 1 + rng.permutation(C - 2)
    n[:, j[:C // 3]] = 0
    n[:, j[C // 3:2 * (C // 3)]] = C - 1
    t = np.stack([paths(rng, n) for r in range(N)])
    for i in range(N):
        r, k = o[i], 2.0 ** 30 if i % 2 == 0 else 2.0 ** -30
        if i % 2 == 0: x[r] = sign * k * (1 - 0.125 * rng.integers(0, 4, (8, 1, C, 1)))
        else: x[r] = sign * k * (1 + 0.125 * rng.integers(0, 8, (8, 1, C, 1)))
        none = 1 + rng.permutation(6)[:2]
        for g in range(8):
            if g in none: continue
            b = -1.0 if i == 0 else 1.0 if i == 2 else rng.choice([-1.0, 1.0])
            u[r, :, 16 * g] = (sign.reshape(128, 4) * (k * b)).astype(np.float32).astype(BF)
        v[r] = rng.choice([-1.0, 1.0], (128, 512)) * k
    t[o[0]] = C - 1
    t[o[1]] = 0
    t[o[2]] = np.where(np.arange(8) % 2 == 1, C - 1, 0)[:, None]
    return {"x": x.astype(np.float32).reshape(N, 128, 4 * C).astype(BF), "u": u.reshape(N, 128, 512), "v": v.astype(np.float32).astype(BF), "nb": np.stack([gtable(n)] * N), "p": np.stack([gtable(t[r]) for r in range(N)]), **weights(rng, range(16))}
def setup_inputs_spread(rng):
    d = setup_inputs(rng)
    d["x"] = big(wide(rng, N, 128, 4 * C, cols=6))
    return d
def check_inputs(d):
    b = []
    for k in ("x", "u", "v"):
        a = np.abs(d[k].astype(np.float32))
        if not (np.isfinite(a).all() and ((a == 0) | (a >= 2.0 ** -30) & (a <= 2.0 ** 30)).all()): b.append("a value of " + k)
    for k in ("nb", "p"):
        if not ((d[k] >= 0) & (d[k] < C)).all(): b.append("an entry of " + k)
    if (d["nb"] != d["nb"][:1]).any(): b.append("nb isn't the same on all ranks")
    none, least, most = [emit(mx_ref.quantize(np.full((128, 16), k, np.float32).astype(BF)))[1][0, 0] for k in (0.0, 2.0 ** -30, 2.0 ** 30)]
    tops = emit(mx_ref.quantize((np.ones((128, 1)) * np.repeat(1 + np.arange(128) * 2.0 ** -7, 4)).astype(np.float32).astype(BF)))[0] & 0x7F
    for r in range(N):
        if ((d["wc"][r] & 0x7F) == 0x7F).any(): b.append("wc: a code that is no number")
        s = mx_ref.live(d["ws"][r])
        if ((s != none) & ((s < least) | (s > most))).any(): b.append("ws: a scale out of range")
        elif not (np.sum(np.abs(decode(pk(d["wc"][r], d["ws"][r])).astype(np.float64)).reshape(128, 512, 4), axis=(0, 2)) <= 32).all(): b.append("the sizes in a column of W")
        a = np.max((d["wc"][r] & 0x7F).reshape(16, 8, 512, 4), axis=(1, 3))
        if not np.where(s == none, a == 0, (a >= np.min(tops)) & (a <= np.max(tops))).all(): b.append("wc: the codes of a block")
    return b
def hop(a, s, n):
    a = np.array(a)
    best = [n[np.argmax(s[e][n], axis=0), np.arange(C)] for e in (0, 7)]
    for h in range(4):
        for g in range(h % 2, 8, 2):
            if g == 0 or g == 7:
                m = a[1] if g == 0 else a[6]
                b = np.where(a[g] == m, best[0 if g == 0 else 1][m], m)
            else:
                low, high = a[g - 1] == a[g], a[g + 1] == a[g]
                b = np.where(low & ~high, a[g + 1], np.where(high & ~low, a[g - 1], a[g]))
            a[g] = np.where(s[g][b] > s[g][a[g]], b, a[g])
    return a
def reference(x, u, v, nb, p, wc, ws):
    qu = [mx_ref.quantize(u[r]) for r in range(N)]
    lay = [pk(wc[r], ws[r]) for r in range(N)]
    now = [x[r] for r in range(N)]
    at = [gentries(p[r]) for r in range(N)]
    for t in range(R):
        have, moved, z, first, gone = [], [], [], [], []
        for r in range(N):
            q = mx_ref.quantize(now[r])
            have.append(decode(q).astype(BF))
            s = mx_ref.matmul(qu[r], q)[::16] + np.float32(0.0)
            a = hop(at[r], s, gentries(nb[r]))
            bond = np.concatenate([a[1:], a[6:7]])
            z.append(((gcols(have[r], a).astype(np.float32) + gcols(have[r], bond).astype(np.float32)) * np.float32(0.5)).astype(BF))
            first.append(np.argsort(-np.sum(a[:-1] != a[1:], axis=0), kind="stable")[:K])
            gone.append(mx_ref.quantize(np.ascontiguousarray(cols(z[r], first[r]))))
            moved.append(a)
        for r in range(N):
            e = (r - 1) % N
            l = tile([mx_ref.matmul(pick(lay[r], np.arange(128 * b, 128 * b + 128)), gone[e]) * np.float32(0.03125) for b in range(4)])
            y = np.array(z[r]).reshape(128, J, 4)
            y[:, first[r]] = l.reshape(128, K, 4)
            at[r] = np.array(moved[r])
            at[r][:, first[r]] = moved[e][:, first[e]]
            low = np.stack([J + np.arange(C)] * 8)
            np.minimum.at(low, (np.arange(8)[:, None], at[r]), np.arange(J)[None])
            w = gcols(np.concatenate([y.reshape(128, 4 * J), have[r]], axis=1), low)
            now[r] = ((have[r].astype(np.float32) + w.astype(np.float32)) * np.float32(0.5)).astype(BF)
    y, ad = np.zeros((N, 128, C), np.float32), np.zeros((N, 8, J), np.float32)
    oc, osc = np.zeros((N, 128, 4 * C), np.uint8), np.zeros((N, 16, C), np.uint8)
    for r in range(N):
        q = mx_ref.quantize(now[r])
        y[r] = mx_ref.matmul(mx_ref.quantize(v[r]), q)
        ad[r] = at[r]
        oc[r], osc[r] = emit(q)
    return {"y": y, "ad": ad, "oc": oc, "osc": osc}

@@ -1,0 +1,527 @@
+from concourse.mybir import dt, AluOpType, AxisListType, ActivationFunctionType
+
+ROUNDS = 3
+BIAS = 8
+F32, BF, I32, U16, MXC, U8 = "float32", "bfloat16", "int32", "uint16", "float8_e4m3fn_x4", "uint8"
+SCRATCH, PART = {}, {}
+
+
+def _sb(dtype, **kw):
+    for k, n in kw.items():
+        SCRATCH[k] = ("sbuf", [128, n], dtype)
+        PART[k] = (k, 0, n)
+
+
+def _pack(buf, dtype, **kw):
+    at = 0
+    for k, n in kw.items():
+        PART[k] = (buf, at, n)
+        at += (n + 15) // 16 * 16
+    SCRATCH[buf] = ("sbuf", [128, at], dtype)
+
+
+_sb(BF, XT=1280, MT=1280, UT=512, VT=512, BY=512, ON=512, DT=512, HT=512, HG=512)
+_pack("CTB", BF, CT0=512, CT1=512, CT2=512, CT3=512)
+_pack("CBB", BF, CB0=512, CB7=512)
+_pack("YW", BF, YW0=960, YW1=960, YW2=960, YW3=960)
+_pack("FH", BF, FH0=320, FH1=320, FH2=320, FH3=320)
+_pack("FQ", BF, FQ0=320, FQ1=320, FQ2=320, FQ3=320)
+_pack("PF", BF, PF0=320, PF1=320, PF2=320, PF3=320)
+_pack("ZG", BF, ZG0=512, ZG1=512, ZG2=512, ZG3=512)
+_sb(MXC, uq=128, ur=1152, vq=128, dq=128, aq=128, wq=512, mq0=320, mq1=320, mq2=320, mq3=320, lq0=320, lq1=320, lq2=320)
+_sb(U8, us=128, urs=1152, vs=128, dsc=128, asc=128, wsc=512, ms0=320, ms1=320, ms2=320, ms3=320, ls0=320, ls1=320, ls2=320)
+_pack("eqc", MXC, eq0=128, eq1=128, eq2=128, eq3=128, bq0=128, bq7=128)
+_pack("esc", U8, es0=128, es1=128, es2=128, es3=128, bs0=128, bs7=128)
+_sb(F32, IOTA=4096, IO512=320, LOWC=672, PLC=512)
+_pack("KC", F32, MASK=512, KEEP=512, ONES=320, JK=4, CE=32, CIDX=20, PCF=4, JKN=32, HN=32)
+_sb(BF, KEEPB=512)
+_sb(I32, CI=512, CJ=32, PCI=4)
+_sb(F32, W07=320, ST=2560, NB8=2560, KT0=640, KT7=640, YO=320)
+_pack("BN", F32, GB=320, M1=160, M2=80, M3=40, NE8=320, SC8=320)
+_sb(I32, LBI=20, NBI=160, PI=32)
+_sb(U16, LB=20, NBL=160, ULU=72)
+SCRATCH["NBD"] = ("dram", [16, 160], I32)
+_pack("HB", F32, RB=32, E=16, O=16, SE=16, SO=16, DA=16, DB=20, SM=16, PR=16, PZ=16, DL=16, KK=16, EQ4=4, KO=4, GT=16, GD=16, R=36, NE=28, D4=4, KR=32, NK=4, TA=96, PS=4, PP=32, PT=32, PF32=32, ISL=32, PD=32, PM=32, SELF=32, FC=32, LZ=32, N1=32, N2=32, OF=32, BI=40, GK=64, SK=64, GS=256, SS=256, GI=512, SI=512, G8=128, S8=128)
+_sb(F32, TR=32, RK=512, SG=512, FW=640, DP=512, SRT=512, SELX=512, FM=512, SCN=512, FX=512, LOWA=672, LOWB=672, LO1=640, LO2=320, REVF=32, XE=320, XS=320, FXR=512)
+_sb(BF, CMP=512, EQB=512, CNT=512)
+_pack("HI", I32, P8=8, P8A=8, P8B=8, XI=20, XJ=20)
+_pack("HU", U16, OFFI=32, KOU=4, KU=16, TU=96, PU=32, SEL=32, EL=20, OFF=32, REV=32, BIU=40)
+_sb(U16, AL=96, PA=32, SL0=16, SL1=16, SL2=16, AR0=16, AR1=16, AR2=16)
+for _t in range(8):
+    SCRATCH["ps%d" % _t] = ("psum", [128, 512], F32)
+
+SEMAPHORES = ["sv", "st", "ss", "sg", "dx", "du", "dv", "dw", "dp", "dlb", "dnb", "dnl", "rsend", "dad", "doc", "dy"]
+for _t in range(3):
+    SEMAPHORES += ["da%d" % _t, "db%d" % _t, "dc%d" % _t, "rq%d" % _t, "rl%d" % _t]
+
+
+def rank_program(g, core, T, topo):
+    rank = T.rank_of(core)
+    if rank is None:
+        return
+    A, ACT = AluOpType, ActivationFunctionType
+    add, sub, mul, mx_, mn_, eq, ne, gt, lt = A.add, A.subtract, A.mult, A.max, A.min, A.is_equal, A.not_equal, A.is_gt, A.is_lt
+    bw, shr = A.bitwise_and, A.arith_shift_right
+    queue = {"v": g.vector, "t": g.tensor, "s": g.scalar, "y": g.sync, "g": g}
+    own = {"v": "sv", "t": "st", "s": "ss", "g": "sg"}
+    count = {k: 0 for k in own}
+    know = {k: {} for k in queue}
+    hist, serial, totals = {}, [0], {}
+
+    def W(name, a, b, st=1, p0=0, p1=128, ps=1):
+        buf, at, _n = PART.get(name, (name, 0, 0))
+        return (buf, a + at, b + at, st, p0, p1, ps)
+
+    def N(v):
+        return W(v, 0, PART[v][2]) if isinstance(v, str) else v
+
+    def I(win, off):
+        return ("I", N(win), N(off))
+
+    def ap(v):
+        v = N(v)
+        if v[0] == "I":
+            return ap(v[1]).indirect(ap(v[2]))
+        n, a, b, st, p0, p1, ps = v
+        rows = slice(p0, p1, ps) if ps != 1 else slice(p0, p1)
+        cs = slice(a, b, st) if st != 1 else slice(a, b)
+        return T[n][rows, cs]
+
+    def meet(a, b, s, c, d, u):
+        if b <= c or d <= a:
+            return False
+        return not (s == u and s > 1 and (a - c) % s)
+
+    def overlap(x, y):
+        return meet(x[1], x[2], x[3], y[1], y[2], y[3]) and meet(x[4], x[5], x[6], y[4], y[5], y[6])
+
+    def covers(x, y):
+        return x[3] == 1 and x[6] == 1 and x[1] <= y[1] and x[2] >= y[2] and x[4] <= y[4] and x[5] >= y[5]
+
+    def sync_for(q, reads, writes):
+        todo = {}
+        for v, w in [(v, False) for v in reads] + [(v, True) for v in writes]:
+            bank = v[0].startswith("ps")
+            for h in hist.get(v[0], ()):
+                if not (w or h["w"] or (bank and h["q"] != q)):
+                    continue
+                if not bank and not overlap(v, h["v"]):
+                    continue
+                if know[q].get(h["sem"], 0) < h["val"]:
+                    if h["sem"] not in todo or todo[h["sem"]]["val"] < h["val"]:
+                        todo[h["sem"]] = h
+        for h in sorted(todo.values(), key=lambda h: -h["n"]):
+            if know[q].get(h["sem"], 0) >= h["val"]:
+                continue
+            queue[q].wait_ge(T.sem[h["sem"]], h["val"])
+            for s, x in h["snap"].items():
+                know[q][s] = max(know[q].get(s, 0), x)
+            know[q][h["sem"]] = h["val"]
+
+    def note(q, reads, writes, sem, val, late, snap=None):
+        serial[0] += 1
+        snap = dict(know[q]) if snap is None else snap
+        for v, w in [(v, False) for v in reads] + [(v, True) for v in writes]:
+            old = hist.setdefault(v[0], [])
+            if w:
+                old[:] = [h for h in old if not covers(v, h["v"])]
+            else:
+                old[:] = [h for h in old if not (not h["w"] and h["q"] == q and not late and not h["late"] and h["v"] == v)]
+            old.append({"v": v, "w": w, "q": q, "late": late, "sem": sem, "val": val, "snap": snap, "n": serial[0]})
+
+    def op(q, call, reads, writes):
+        rd, wr = [], []
+        for v in map(N, reads):
+            rd += [v[1], v[2]] if v[0] == "I" else [v]
+        for v in map(N, writes):
+            wr.append(v[1] if v[0] == "I" else v)
+            rd += [v[2]] if v[0] == "I" else []
+        sync_for(q, rd, wr)
+        if q == "g" and know[q].get("sg", 0) < count[q]:
+            g.wait_ge(T.sem["sg"], count[q])
+            know[q]["sg"] = count[q]
+        count[q] += 1
+        call().then_inc(T.sem[own[q]], 1)
+        note(q, rd, wr, own[q], count[q], False)
+
+    def cp(out, a):
+        op("v", lambda: g.vector.tensor_copy(ap(out), ap(a)), [a], [out])
+
+    def tt(out, a, b, o):
+        op("v", lambda: g.vector.tensor_tensor(ap(out), ap(a), ap(b), o), [a, b], [out])
+
+    def ts(out, a, s1, o0, s2=None, o1=None):
+        x1, x2 = [ap(s) if isinstance(s, tuple) else s for s in (s1, s2)]
+        more = () if o1 is None else (o1,)
+        op("v", lambda: g.vector.tensor_scalar(ap(out), ap(a), x1, x2, o0, *more), [a] + [s for s in (s1, s2) if isinstance(s, tuple)], [out])
+
+    def scan(out, d0, d1):
+        op("v", lambda: g.vector.tensor_tensor_scan(ap(out), ap(d0), ap(d1), 0.0, mul, add), [d0, d1], [out])
+
+    def red(out, a):
+        op("v", lambda: g.vector.tensor_reduce(ap(out), ap(a), AxisListType.X, add), [a], [out])
+
+    def fill(out, c):
+        op("v", lambda: g.vector.memset(ap(out), c), [], [out])
+
+    def tr(out, a):
+        op("v", lambda: g.vector.transpose(ap(out), ap(a)), [a], [out])
+
+    def quant(q, s, a):
+        op("v", lambda: g.vector.quantize_mx(ap(q), ap(s), ap(a)), [a], [q, s])
+
+    def act(out, a, scale=1.0):
+        more = {} if scale == 1.0 else {"scale": scale}
+        op("s", lambda: g.scalar.activation(ap(out), ap(a), ACT.Copy, **more), [a], [out])
+
+    def iota(out, pattern, base, mult):
+        more = {"allow_small_or_imprecise_dtypes": True} if SCRATCH[N(out)[0]][2] == F32 else {}
+        op("g", lambda: g.iota(ap(out), pattern, base, mult, **more), [], [out])
+
+    def select(out, a, pattern, base, mult):
+        op("g", lambda: g.affine_select(ap(out), ap(a), pattern, eq, 0.0, base, mult), [a], [out])
+
+    def mm(bank, lq, ls, l0, rq, rs):
+        a, b, o = W(lq, l0, l0 + 128), W(ls, l0, l0 + 128), W("ps%d" % bank, 0, PART[rq][2])
+        op("t", lambda: g.tensor.matmul_mx(ap(o), ap(a), ap(b), ap(rq), ap(rs), True, True), [a, b, rq, rs], [o])
+
+    def dmas(sem, items):
+        done, total = [], 16 * len(items)
+        totals[sem] = total
+
+        def side(v):
+            if isinstance(v, tuple) and v[0] == "C":
+                return ap(v[1]).bitcast(dt.uint8), [N(v[1])]
+            return (ap(v), [N(v)]) if isinstance(v, (tuple, str)) else (v, [])
+        for q, out, a in items:
+            (o, ow), (i, ir) = side(out), side(a)
+            sync_for(q, ir, ow)
+            queue[q].dma_start(o, i).then_inc(T.sem[sem], 16)
+            done.append((q, ir, ow, dict(know[q])))
+        for q, ir, ow, snap in done:
+            note(q, ir, ow, sem, total, True, snap)
+
+    nxt, prv = T.cores[(rank + 1) % len(T.cores)], T.cores[(rank - 1) % len(T.cores)]
+    a_nxt, m_nxt = topo.addr(nxt), topo.mask(core, nxt)
+    e_out, e_in = len(topo.engines(core, nxt)), len(topo.engines(prv, core))
+    sent = [0]
+
+    def send(out, src, rsem, code=False):
+        sync_for("g", [N(src)], [])
+        o, i = ap(out), ap(src)
+        if code:
+            o, i = o.bitcast(dt.uint8), i.bitcast(dt.uint8)
+        g.remote_dma(o, i, T.sem[rsem], T.sem["rsend"], a_nxt[1], a_nxt[0], m_nxt)
+        sent[0] += e_out
+
+    def arrival(names, sem, n):
+        totals[sem] = n
+        note("r", [], [N(v) for v in names], sem, n, True, {})
+
+    dmas("dx", [("y", "XT", T.x[:, :])])
+    dmas("du", [("s", "UT", T.u[:, :])])
+    dmas("dlb", [("ys"[t % 2], W("LBI", 0, 20, 1, 8 * y + 7 - t, 128, 16), T.nb[16 * t + 8 * y:16 * t + 8 * y + 8, :]) for y in range(2) for t in range(8)])
+    dmas("dp", [("ys"[(b + Q) % 2], W("PI", 0, 32, 1, 32 * Q + b, 32 * Q + 32, 4), T.p[15 - 4 * b - Q:128:16, :]) for Q in range(4) for b in range(4)])
+    dmas("dnb", [("ys"[k % 2], W("NBD", 20 * k, 20 * k + 20, 1, 8 * y, 8 * y + 8), T.nb[2 * k + y:128:16, :]) for k in range(8) for y in range(2)])
+    dmas("dnl", [("y", W("NBI", 0, 160, 1, 16 * k, 16 * k + 16), W("NBD", 0, 160, 1, 0, 16)) for k in range(8)])
+    dmas("dw", [("y", ("C", "wq"), T.wc[:, :]), ("y", "wsc", T.ws[:, :])])
+    dmas("dv", [("y", "VT", T.v[:, :])])
+
+    fill("BY", 0.0)
+    for k in range(8):
+        for y in range(2):
+            fill(W("BY", 64 * k + 33 * y, 64 * k + 32 * y + 32, 4), 1.0)
+    fill("ULU", 0)
+    fill("DT", 0.0)
+    iota(W("PCI", 0, 1), [[0, 1]], 0, 1)
+    iota(W("IOTA", 0, 320), [[1, 320]], 0, 0)
+    for e in (0, 7):
+        select("CB%d" % e, "BY", [[0, 16], [-16, 8], [0, 4]], 0 if e == 0 else -8, 1)
+    iota("CI", [[0, 32], [-1, 16]], 16, 1)
+    iota("CIDX", [[16, 20]], -1, 0)
+    for Q in range(4):
+        iota(W("JK", 0, 4, 1, 32 * Q, 32 * Q + 32), [[-4, 4]], 7 * 512 + 15 - Q, 16)
+    iota("CE", [[16, 32]], 128, 0)
+    iota("CJ", [[16, 32]], 15, 0)
+    for kt in ("KT0", "KT7"):
+        act(W(kt, 0, 320), W("IOTA", 0, 320))
+
+    def later_constants():
+        for b in range(4):
+            select("CT%d" % b, "ON", [[1, 512]], -b, -4)
+        iota(W("LOWC", 0, 336), [[1, 336]], 512 * 1024 + 640, 0)
+        iota(W("LOWC", 336, 672), [[1, 336]], 512 * 1024 + 640, 0)
+        iota("PLC", [[16384, 32], [-1024, 16]], 15 * 1024, 0)
+        iota("IO512", [[512, 320]], 0, 0)
+        iota(W("IOTA", 320, 4096), [[1, 3776]], 320, 0)
+
+    pc, pf = (lambda i: W("PCI", i, i + 1)), (lambda i: W("PCF", i, i + 1))
+    ts(pc(1), pc(0), 15, bw)
+    ts(pc(2), pc(0), 3, shr, 1, bw)
+    cp(pf(0), pc(1))
+    cp(pf(1), pc(2))
+    ts(W("ULU", 0, 8), W("ULU", 8, 16), pf(1), add, 112.0, mul)
+    for k in range(1, 8):
+        fill(W("ULU", 8 + 8 * k, 16 + 8 * k), 16 * k)
+    quant("uq", "us", "UT")
+
+    def pick_u(a, b):
+        ul, o = W("ULU", a // 16, b // 16), W("ur", a, b)
+        op("v", lambda: g.vector.tensor_copy(ap(o).bitcast(dt.uint32), ap("uq").bitcast(dt.uint32).indirect(ap(ul))), ["uq", ul], [o])
+        act(W("urs", a, b), I("us", ul))
+    pick_u(0, 128)
+    quant("mq0", "ms0", "XT")
+    pick_u(128, 1152)
+    for e in (0, 7):
+        quant("bq%d" % e, "bs%d" % e, "CB%d" % e)
+    fill("ONES", 1.0)
+    fill("ON", 1.0)
+    cp("LB", "LBI")
+    ts("TR", "PI", float(BIAS), add)
+    CELLS, CELLS8 = W("IOTA", 0, 320), W("IOTA", BIAS, BIAS + 320)
+
+    def more_constants():
+        cp("NBL", "NBI")
+        act(W("NB8", 0, 1600), I(CELLS, W("NBL", 0, 100)))
+        fill("DB", 0.0)
+        for k in ("KEEP", "KEEPB"):
+            fill(k, 1.0)
+        for k in ("KEEP", "KEEPB"):
+            fill(W(k, 0, 512, 16), 0.0)
+        ts("CI", "CI", 15, bw)
+        ts("MASK", "CI", 0.0, eq)
+        ts("CE", "CE", pf(0), add)
+        ts(pc(2), pc(1), 1, shr)
+        ts(pc(3), pc(1), 1, bw)
+        ts(pf(2), pc(2), 320.0, mul)
+        ts(pf(3), pc(3), 8.0, mul)
+        ts("CIDX", "CIDX", pf(2), add, pf(3), add)
+        ts(pf(0), pf(0), 320.0 + BIAS, add)
+        cp(W("NB8", 1600, 2560), I(CELLS, W("NBL", 100, 160)))
+
+    def last_constants():
+        for b in range(4):
+            quant("eq%d" % b, "es%d" % b, "CT%d" % b)
+        for k in range(8):
+            ts(W("JKN", 4 * k, 4 * k + 4), "JK", -1.0 / 512, mul)
+        fill("HN", -511.0)
+        fill(W("HN", 3, 32, 4), 0.0)
+
+    def end_constants():
+        quant("vq", "vs", "VT")
+        ts("REVF", "CJ", pf(0), sub, 320.0 + BIAS, add)
+        cp("REV", "REVF")
+
+    MASK, KEEP = (lambda n: W("MASK", 0, n)), (lambda n: W("KEEP", 0, n))
+
+    def halfstep(par, last, fillers):
+        Y, S = ("E", "SE") if par == 0 else ("O", "SO")
+        eb, i0 = (0, 4) if par == 0 else (12, 0)
+        ge, kt = (0, "KT0") if par == 0 else (7, "KT7")
+        m = W("O", 0, 4) if par == 0 else W("E", 12, 16)
+        dbv = W("DB", 0, 16) if par == 0 else W("DB", 4, 20)
+        tt("DA", "O", "E", sub)
+        tt(W("DB", 4, 16), W("E", 4, 16), W("O", 0, 12), sub)
+        ts("EQ4", W("DA", eb, eb + 4), 0.0, eq, 320.0, mul)
+        tt("PR", "DA", dbv, mul)
+        if par == 0:
+            tt("SM", "DA", dbv, sub)
+        else:
+            tt("SM", dbv, "DA", sub)
+        tt("KO", "EQ4", m, add)
+        ts("PZ", "PR", 0.0, eq)
+        cp("KOU", "KO")
+        tt("DL", "SM", "PZ", mul)
+        tt("GK", I(kt, "KOU"), MASK(64), mul)
+        tt("KK", Y, "DL", add)
+        for i in range(i0 // 4, i0 // 4 + 3):
+            ts(W("KU", 4 * i, 4 * i + 4), W("KK", 4 * i, 4 * i + 4), 320.0 * (2 * i + par), add)
+        scan("SK", KEEP(64), "GK")
+        gi, si = W("GS", 16 * i0, 16 * i0 + 192), W("SS", 16 * i0, 16 * i0 + 192)
+        tt(gi, I("ST", W("KU", i0, i0 + 12)), MASK(192), mul)
+        k0 = W("SK", 15, 64, 16)
+        ts(W("KU", eb, eb + 4), k0, 320.0 * ge, add)
+        tt(W("DL", eb, eb + 4), k0, W(Y, eb, eb + 4), sub)
+        scan(si, KEEP(192), gi)
+        gi, si = W("GS", 16 * eb, 16 * eb + 64), W("SS", 16 * eb, 16 * eb + 64)
+        tt(gi, I("ST", W("KU", eb, eb + 4)), MASK(64), mul)
+        for f in fillers:
+            f()
+        scan(si, KEEP(64), gi)
+        sk = W("SS", 15, 256, 16)
+        tt("GT", sk, S, gt)
+        if not last:
+            tt(S, sk, S, mx_)
+        tt("GD", "GT", "DL", mul)
+        if last and par == 1:
+            for i in range(4):
+                tt(W("R", 8 * i + 4, 8 * i + 8), W("O", 4 * i, 4 * i + 4), W("GD", 4 * i, 4 * i + 4), add)
+        else:
+            tt(Y, Y, "GD", add)
+
+    for rd in range(ROUNDS):
+        mq, ms, lq, ls, sl, ar = "mq%d" % rd, "ms%d" % rd, "lq%d" % rd, "ls%d" % rd, "SL%d" % rd, "AR%d" % rd
+        send(lq, mq, "rq%d" % rd, True)
+        send(ls, ms, "rq%d" % rd)
+        arrival([lq, ls], "rq%d" % rd, 2 * e_in)
+        if rd == 0:
+            later_constants()
+        mm(0, "ur", "urs", 0, mq, ms)
+        for k in range(8):
+            mm((k + 1) % 8, "ur", "urs", 128 + 128 * k, mq, ms)
+            if k == 0:
+                act("W07", W("ps0", 0, 320))
+            act(W("ST", 320 * k, 320 * k + 320), W("ps%d" % ((k + 1) % 8), 0, 320))
+        tr("RB", "TR")
+        for i in range(4):
+            for par in range(2):
+                src = W("RB", 8 * i + 4 * par, 8 * i + 4 * par + 4)
+                ts(W("OFFI", 16 * par + 4 * i, 16 * par + 4 * i + 4), src, 320.0 * (2 * i + par) - BIAS, add)
+                ts(W("EO"[par], 4 * i, 4 * i + 4), src, -float(BIAS), add)
+        cp("GB", I("W07", "LB"))
+        tt("M1", W("GB", 0, 320, 2), W("GB", 1, 320, 2), mx_)
+        tt("M2", W("M1", 0, 160, 2), W("M1", 1, 160, 2), mx_)
+        tt("M3", W("M2", 0, 80, 2), W("M2", 1, 80, 2), mx_)
+        for t in range(8):
+            tt(W("NE8", t, 320, 8), W("GB", t, 320, 8), "M3", ne)
+        scan("SC8", "NE8", "ONES")
+        cp(W("DT", 0, 80, 4), W("SC8", 7, 320, 16))
+        cp(W("DT", 1, 80, 4), W("SC8", 15, 320, 16))
+        quant("dq", "dsc", "DT")
+        mm(1, "bq0", "bs0", 0, "dq", "dsc")
+        mm(2, "bq7", "bs7", 0, "dq", "dsc")
+        if rd == 0:
+            more_constants()
+        tt(W("BI", 0, 20), W("ps1", 0, 20), "CIDX", add)
+        tt(W("BI", 20, 40), W("ps2", 0, 20), "CIDX", add)
+        cp("BIU", "BI")
+        act(W("KT0", 320, 640), I("NB8", W("BIU", 0, 20)))
+        act(W("KT7", 320, 640), I("NB8", W("BIU", 20, 40)))
+        tt("GI", I("ST", "OFFI"), "MASK", mul)
+        scan("SI", "KEEP", "GI")
+        cp("SE", W("SI", 15, 256, 16))
+        cp("SO", W("SI", 271, 512, 16))
+        halfstep(0, False, [])
+        if rd == 0:
+            last_constants()
+        for t in range(4):
+            f = W("ps%d" % (3 + t), 0, 320)
+            mm(3 + t, "eq%d" % t, "es%d" % t, 0, mq, ms)
+            act("FQ%d" % t, f, 0.25)
+            act("FH%d" % t, f, 0.5)
+            act(W("YW%d" % t, 640, 960), f, 0.5)
+        act("LOWA", "LOWC")
+        act("LOWB", "LOWC")
+        for t in range(4):
+            k = (7, 0, 1, 2)[t]
+            mm(k, "eq%d" % t, "es%d" % t, 0, lq, ls)
+            act("PF%d" % t, W("ps%d" % k, 0, 320), 0.5)
+        halfstep(1, False, [])
+        halfstep(0, True, [])
+        halfstep(1, True, [lambda i=i: cp(W("R", 8 * i, 8 * i + 4), W("E", 4 * i, 4 * i + 4)) for i in range(4)] + [lambda: cp(W("R", 32, 36), W("E", 12, 16))])
+        tt("NE", W("R", 0, 28), W("R", 4, 32), ne)
+        tr(W("TA", 0, 32), W("R", 0, 32))
+        tr(W("TA", 32, 64), W("R", 4, 36))
+        for b in range(4):
+            red(W("D4", b, b + 1), W("NE", b, 28, 4))
+        for b in range(4):
+            ts(W("KR", b, 32, 4), W("JKN", b, 32, 4), W("D4", b, b + 1), add, -512.0, mul)
+        tr(W("TA", 64, 96), "KR")
+        ts("NK", W("KR", 0, 4), -1.0, mul)
+        cp("TU", "TA")
+        dmas("da%d" % rd, [("ys"[Q % 2], W("AL", 0, 96, 1, Q, 128, 4), W("TU", 0, 96, 1, 32 * Q, 32 * Q + 32)) for Q in range(4)])
+        if rd == 0:
+            end_constants()
+        al, bl, kl = W("AL", 0, 32), W("AL", 32, 64), W("AL", 64, 96)
+        cp("RK", I("IOTA", kl))
+        for b in range(3):
+            bi, ac = W("NK", b, b + 1), W("PS", b, b + 1)
+            op("s", lambda: g.scalar.activation(ap("SG"), ap("RK"), ACT.Sign, bias=ap(bi), accum_out=ap(ac)), ["RK", bi], ["SG", ac])
+        act(W("FW", 128, 640), I(CELLS8, al))
+        ts("CMP", "RK", W("KR", 3, 4), lt, -2.0, mul)
+        red(W("PS", 3, 4), "CMP")
+        for b in range(4):
+            ts(W("PP", b, 32, 4), W("HN", b, 32, 4), W("PS", b, b + 1), add, -0.5, mul)
+        tr("PT", "PP")
+        cp("PU", "PT")
+        dmas("db%d" % rd, [("y", W("PA", 0, 32, 1, Q, 128, 4), W("PU", 0, 32, 1, 32 * Q, 32 * Q + 32)) for Q in range(4)])
+        tt("DP", I("IO512", bl), W("FW", 128, 640), add)
+        for t in range(4):
+            act("ZG%d" % t, I("FQ%d" % t, al))
+
+        def bonds(t):
+            tt(W("YW%d" % t, 128, 640), I("FQ%d" % t, bl), "ZG%d" % t, add)
+        bonds(0)
+        bonds(1)
+        cp(I("SRT", "PA"), "DP")
+        cp("PF32", "PA")
+        tt("G8", W("SRT", 0, 128), MASK(128), mul)
+        ts("ISL", "PF32", 128.0, lt)
+        scan("S8", KEEP(128), "G8")
+        tt("PD", "PF32", "CE", sub)
+        cp("P8", W("S8", 15, 128, 16))
+        tt("PM", "PD", "ISL", mul)
+        ts("P8A", "P8", 511, bw)
+        ts("P8B", "P8", 9, shr)
+        tt("SELF", "PM", "CE", add)
+        ts(W(sl, 0, 8), "P8A", -float(BIAS), add)
+        cp(W(sl, 8, 16), "P8B")
+        cp("SEL", "SELF")
+        send(ar, sl, "rl%d" % rd)
+        arrival([ar], "rl%d" % rd, e_in)
+        tt("SELX", I("IOTA", "SEL"), "PLC", add)
+        bonds(2)
+        bonds(3)
+        aa, ab = W(ar, 0, 8), W(ar, 8, 16)
+        cp(W("FW", 0, 128), I(CELLS8, aa))
+        for t in range(4):
+            act(W("HG", 128 * t, 128 * t + 128), I("PF%d" % t, aa))
+        act("FX", I("FW", "SEL"))
+        tt("FM", I("FW", "SEL"), "MASK", mul)
+        for t in range(4):
+            tt(W("HT", t, 512, 4), I("PF%d" % t, ab), W("HG", 128 * t, 128 * t + 128), add)
+        scan("SCN", "KEEP", "FM")
+        quant("aq", "asc", "HT")
+        for b in range(4):
+            mm(3 + b, "wq", "wsc", 128 * b, "aq", "asc")
+            act(W("YW%d" % b, 0, 128), W("ps%d" % (3 + b), 0, 128), 2.0 ** -6)
+        if rd + 1 == ROUNDS:
+            fr = I("FX", "REV")
+            op("s", lambda: g.scalar.activation(ap("FXR"), ap(fr), ACT.Identity, bias=-float(BIAS)), [fr], ["FXR"])
+            dmas("dad", [("y", T.ad[:, :], W("FXR", 0, 512, 1, 0, 128, 16))])
+        tt("EQB", "FX", "SCN", eq)
+        cp("FC", W("SCN", 15, 512, 16))
+        if rd + 1 < ROUNDS:
+            dmas("dc%d" % rd, [("y", W("TR", 0, 32, 1, 32 * Q, 32 * Q + 32), W("FC", 0, 32, 1, Q, 128, 4)) for Q in range(4)])
+        scan("CNT", "KEEPB", "EQB")
+        ts("N1", "FC", -1.0, mul, pf(0), add)
+        ts("LZ", W("CNT", 15, 512, 16), 1.5, gt)
+        tt("N2", "LZ", "N1", mul)
+        tt("OF", "FC", "N2", add)
+        ts(W("OFF", 0, 32, 2), W("OF", 0, 32, 2), -float(BIAS), add)
+        ts(W("OFF", 1, 32, 2), W("OF", 1, 32, 2), 336.0 - BIAS, add)
+        for k in range(15, -1, -1):
+            cp(I("LOWA" if k % 2 else "LOWB", W("OFF", 2 * k, 2 * k + 2)), W("SELX", 32 * k, 32 * k + 32))
+        for i in range(2):
+            tt(W("LO1", 320 * i, 320 * i + 320), W("LOWA", 336 * i, 336 * i + 320), W("LOWB", 336 * i, 336 * i + 320), mn_)
+        tt("LO2", W("LO1", 0, 320), W("LO1", 320, 640), mn_)
+        tt("XE", "LO2", MASK(320), mul)
+        scan("XS", KEEP(320), "XE")
+        cp("XI", W("XS", 15, 320, 16))
+        ts("XJ", "XI", 1023, bw)
+        cp("EL", "XJ")
+        for t in range(4):
+            tt(W("MT", t, 1280, 4), I("YW%d" % t, "EL"), "FH%d" % t, add)
+        quant("mq%d" % (rd + 1), "ms%d" % (rd + 1), "MT")
+
+    mq, ms = "mq%d" % ROUNDS, "ms%d" % ROUNDS
+    mm(0, "vq", "vs", 0, mq, ms)
+    act("YO", W("ps0", 0, 320))
+    dmas("doc", [("y", T.oc[:, :], ("C", mq))] + [("y", T.osc[4 * k:4 * k + 4, :], W(ms, 0, 320, 1, 32 * k, 32 * k + 4)) for k in range(4)])
+    dmas("dy", [("s", T.y[:, :], "YO")])
+
+    g.wait_ge(T.sem["rsend"], sent[0])
+    for q in own:
+        g.wait_ge(T.sem[own[q]], count[q])
+    for s in sorted(totals):
+        g.wait_ge(T.sem[s], totals[s])

@@ -1,6 +1,7 @@
 from concourse.mybir import dt, AluOpType, AxisListType, ActivationFunctionType
 
 ROUNDS = 3
+FAR = 1e29
 BIAS = 8
 F32, BF, I32, U16, MXC, U8 = "float32", "bfloat16", "int32", "uint16", "float8_e4m3fn_x4", "uint8"
 SCRATCH, PART = {}, {}
@@ -36,16 +37,16 @@ _sb(F32, IOTA=4096, IO512=320, LOWC=672, PLC=512)
 _pack("KC", F32, MASK=512, KEEP=512, ONES=320, JK=4, CE=32, CIDX=20, PCF=4, JKN=32, HN=32)
 _sb(BF, KEEPB=512)
 _sb(I32, CI=512, CJ=32, PCI=4)
-_sb(F32, W07=320, ST=2560, NB8=2560, KT0=640, KT7=640, YO=320)
+_sb(F32, W07=320, ST=3200, NB8=2560, KT0=320, KT7=320, YO=320)
 _pack("BN", F32, GB=320, M1=160, M2=80, M3=40, NE8=320, SC8=320)
 _sb(I32, LBI=20, NBI=160, PI=32)
 _sb(U16, LB=20, NBL=160, ULU=72)
 SCRATCH["NBD"] = ("dram", [16, 160], I32)
-_pack("HB", F32, RB=32, E=16, O=16, SE=16, SO=16, DA=16, DB=20, SM=16, PR=16, PZ=16, DL=16, KK=16, EQ4=4, KO=4, GT=16, GD=16, R=36, NE=28, D4=4, KR=32, NK=4, TA=96, PS=4, PP=32, PT=32, PF32=32, ISL=32, PD=32, PM=32, SELF=32, FC=32, LZ=32, N1=32, N2=32, OF=32, BI=40, GK=64, SK=64, GS=256, SS=256, GI=512, SI=512, G8=128, S8=128)
+_pack("HB", F32, RB=32, E=16, O=16, SE=16, SO=16, DA=16, DB=20, SM=16, PR=16, NV=16, SYV=16, SG1=16, KK=16, E4=4, SYE=4, KD=4, GTB=4, G2=4, SG2=4, GT=16, GD=16, R=36, NE=28, D4=4, KR=32, NK=4, TA=96, PS=4, PP=32, PT=32, PF32=32, ISL=32, PD=32, PM=32, SELF=32, FC=32, LZ=32, OF=32, BI=40, GK=64, SK=64, GB2=64, SB=64, GS=256, SS=256, GI=512, SI=512, G8=128, S8=128)
 _sb(F32, TR=32, RK=512, SG=512, FW=640, DP=512, SRT=512, SELX=512, FM=512, SCN=512, FX=512, LOWA=672, LOWB=672, LO1=640, LO2=320, REVF=32, XE=320, XS=320, FXR=512)
 _sb(BF, CMP=512, EQB=512, CNT=512)
 _pack("HI", I32, P8=8, P8A=8, P8B=8, XI=20, XJ=20)
-_pack("HU", U16, OFFI=32, KOU=4, KU=16, TU=96, PU=32, SEL=32, EL=20, OFF=32, REV=32, BIU=40)
+_pack("HU", U16, OFFI=32, KOU=4, KU=16, KU2=4, TU=96, PU=32, SEL=32, EL=20, OFF=32, REV=32, BIU=40)
 _sb(U16, AL=96, PA=32, SL0=16, SL1=16, SL2=16, AR0=16, AR1=16, AR2=16)
 for _t in range(8):
     SCRATCH["ps%d" % _t] = ("psum", [128, 512], F32)
@@ -243,8 +244,6 @@ def rank_program(g, core, T, topo):
         iota(W("JK", 0, 4, 1, 32 * Q, 32 * Q + 32), [[-4, 4]], 7 * 512 + 15 - Q, 16)
     iota("CE", [[16, 32]], 128, 0)
     iota("CJ", [[16, 32]], 15, 0)
-    for kt in ("KT0", "KT7"):
-        act(W(kt, 0, 320), W("IOTA", 0, 320))
 
     def later_constants():
         for b in range(4):
@@ -283,18 +282,20 @@ def rank_program(g, core, T, topo):
     def more_constants():
         cp("NBL", "NBI")
         act(W("NB8", 0, 1600), I(CELLS, W("NBL", 0, 100)))
-        fill("DB", 0.0)
         for k in ("KEEP", "KEEPB"):
             fill(k, 1.0)
+        ts("CI", "CI", 15, bw)
         for k in ("KEEP", "KEEPB"):
             fill(W(k, 0, 512, 16), 0.0)
-        ts("CI", "CI", 15, bw)
         ts("MASK", "CI", 0.0, eq)
         ts("CE", "CE", pf(0), add)
         ts(pc(2), pc(1), 1, shr)
         ts(pc(3), pc(1), 1, bw)
+        fill("DB", 0.0)
         ts(pf(2), pc(2), 320.0, mul)
         ts(pf(3), pc(3), 8.0, mul)
+        for k in (0, 2880):
+            fill(W("ST", k, k + 320), 0.0)
         ts("CIDX", "CIDX", pf(2), add, pf(3), add)
         ts(pf(0), pf(0), 320.0 + BIAS, add)
         cp(W("NB8", 1600, 2560), I(CELLS, W("NBL", 100, 160)))
@@ -315,49 +316,60 @@ def rank_program(g, core, T, topo):
     MASK, KEEP = (lambda n: W("MASK", 0, n)), (lambda n: W("KEEP", 0, n))
 
     def halfstep(par, last, fillers):
-        Y, S = ("E", "SE") if par == 0 else ("O", "SO")
-        eb, i0 = (0, 4) if par == 0 else (12, 0)
-        ge, kt = (0, "KT0") if par == 0 else (7, "KT7")
-        m = W("O", 0, 4) if par == 0 else W("E", 12, 16)
-        dbv = W("DB", 0, 16) if par == 0 else W("DB", 4, 20)
-        tt("DA", "O", "E", sub)
-        tt(W("DB", 4, 16), W("E", 4, 16), W("O", 0, 12), sub)
-        ts("EQ4", W("DA", eb, eb + 4), 0.0, eq, 320.0, mul)
-        tt("PR", "DA", dbv, mul)
+        Y, S, oth = ("E", "SE", "O") if par == 0 else ("O", "SO", "E")
+        eb, i0, ge, kt = (0, 4, 0, "KT0") if par == 0 else (12, 0, 7, "KT7")
+        e = lambda n: W(n, eb, eb + 4)
+        m, dbv, off = e(oth), (W("DB", 0, 16) if par == 0 else W("DB", 4, 20)), 320.0 * (ge + 1)
+        cp("KOU", m)
+        ts(e("KU"), m, off, add)
         if par == 0:
-            tt("SM", "DA", dbv, sub)
+            tt(W("KK", 4, 16), W("O", 4, 16), W("DB", 4, 16), sub)
         else:
-            tt("SM", dbv, "DA", sub)
-        tt("KO", "EQ4", m, add)
-        ts("PZ", "PR", 0.0, eq)
-        cp("KOU", "KO")
-        tt("DL", "SM", "PZ", mul)
+            tt(W("KK", 0, 12), W("E", 4, 16), W("DA", 0, 12), sub)
+        tt("PR", "DA", dbv, mul)
+        ts("E4", e("DA"), 0.0, ne, FAR, mul)
         tt("GK", I(kt, "KOU"), MASK(64), mul)
-        tt("KK", Y, "DL", add)
         for i in range(i0 // 4, i0 // 4 + 3):
-            ts(W("KU", 4 * i, 4 * i + 4), W("KK", 4 * i, 4 * i + 4), 320.0 * (2 * i + par), add)
+            ts(W("KU", 4 * i, 4 * i + 4), W("KK", 4 * i, 4 * i + 4), 320.0 * (2 * i + par + 1), add)
+        ts("NV", "PR", 0.0, ne, FAR, mul)
+        tt("SYE", e(S), "E4", add)
         scan("SK", KEEP(64), "GK")
-        gi, si = W("GS", 16 * i0, 16 * i0 + 192), W("SS", 16 * i0, 16 * i0 + 192)
-        tt(gi, I("ST", W("KU", i0, i0 + 12)), MASK(192), mul)
-        k0 = W("SK", 15, 64, 16)
-        ts(W("KU", eb, eb + 4), k0, 320.0 * ge, add)
-        tt(W("DL", eb, eb + 4), k0, W(Y, eb, eb + 4), sub)
-        scan(si, KEEP(192), gi)
-        gi, si = W("GS", 16 * eb, 16 * eb + 64), W("SS", 16 * eb, 16 * eb + 64)
-        tt(gi, I("ST", W("KU", eb, eb + 4)), MASK(64), mul)
+        tt("GS", I("ST", "KU"), MASK(256), mul)
+        tt("SM", *(("DA", dbv) if par == 0 else (dbv, "DA")), sub)
+        tt("SYV", S, "NV", add)
         for f in fillers:
             f()
-        scan(si, KEEP(64), gi)
-        sk = W("SS", 15, 256, 16)
-        tt("GT", sk, S, gt)
-        if not last:
-            tt(S, sk, S, mx_)
-        tt("GD", "GT", "DL", mul)
+        k0, sk, sb = W("SK", 15, 64, 16), W("SS", 15, 256, 16), W("SB", 15, 64, 16)
+        ts("KU2", k0, off, add)
+        scan("SS", KEEP(256), "GS")
+        tt("KD", k0, m, sub)
+        tt("GB2", I("ST", "KU2"), MASK(64), mul)
+        tt("GT", sk, "SYV", gt)
+        scan("SB", KEEP(64), "GB2")
+        tt("GD", "GT", "SM", mul)
+        tt("GTB", sb, "SYE", gt)
         if last and par == 1:
-            for i in range(4):
+            for i in (3, 0, 1, 2):
                 tt(W("R", 8 * i + 4, 8 * i + 8), W("O", 4 * i, 4 * i + 4), W("GD", 4 * i, 4 * i + 4), add)
         else:
             tt(Y, Y, "GD", add)
+            tt("DA", "DA", "GD", sub if par == 0 else add)
+            if par == 0:
+                tt(W("DB", 4, 16), W("DB", 4, 16), W("GD", 4, 16), add)
+            else:
+                tt(W("DB", 4, 16), W("DB", 4, 16), W("GD", 0, 12), sub)
+        tt("G2", "GTB", "KD", mul)
+        if not last:
+            tt("SG1", sk, "NV", sub)
+            tt("SG2", sb, "E4", sub)
+            tt(S, S, "SG1", mx_)
+        if last and par == 1:
+            tt(W("R", 28, 32), W("R", 28, 32), "G2", add)
+        else:
+            tt(e("DA"), e("DA"), "G2", sub if par == 0 else add)
+            tt(e(Y), e(Y), "G2", add)
+        if not last:
+            tt(e(S), e(S), "SG2", mx_)
 
     for rd in range(ROUNDS):
         mq, ms, lq, ls, sl, ar = "mq%d" % rd, "ms%d" % rd, "lq%d" % rd, "ls%d" % rd, "SL%d" % rd, "AR%d" % rd
@@ -371,12 +383,12 @@ def rank_program(g, core, T, topo):
             mm((k + 1) % 8, "ur", "urs", 128 + 128 * k, mq, ms)
             if k == 0:
                 act("W07", W("ps0", 0, 320))
-            act(W("ST", 320 * k, 320 * k + 320), W("ps%d" % ((k + 1) % 8), 0, 320))
+            act(W("ST", 320 * k + 320, 320 * k + 640), W("ps%d" % ((k + 1) % 8), 0, 320))
         tr("RB", "TR")
         for i in range(4):
             for par in range(2):
                 src = W("RB", 8 * i + 4 * par, 8 * i + 4 * par + 4)
-                ts(W("OFFI", 16 * par + 4 * i, 16 * par + 4 * i + 4), src, 320.0 * (2 * i + par) - BIAS, add)
+                ts(W("OFFI", 16 * par + 4 * i, 16 * par + 4 * i + 4), src, 320.0 * (2 * i + par + 1) - BIAS, add)
                 ts(W("EO"[par], 4 * i, 4 * i + 4), src, -float(BIAS), add)
         cp("GB", I("W07", "LB"))
         tt("M1", W("GB", 0, 320, 2), W("GB", 1, 320, 2), mx_)
@@ -392,13 +404,15 @@ def rank_program(g, core, T, topo):
         mm(2, "bq7", "bs7", 0, "dq", "dsc")
         if rd == 0:
             more_constants()
+        tt("GI", I("ST", "OFFI"), "MASK", mul)
         tt(W("BI", 0, 20), W("ps1", 0, 20), "CIDX", add)
         tt(W("BI", 20, 40), W("ps2", 0, 20), "CIDX", add)
         cp("BIU", "BI")
-        act(W("KT0", 320, 640), I("NB8", W("BIU", 0, 20)))
-        act(W("KT7", 320, 640), I("NB8", W("BIU", 20, 40)))
-        tt("GI", I("ST", "OFFI"), "MASK", mul)
+        act("KT0", I("NB8", W("BIU", 0, 20)))
+        act("KT7", I("NB8", W("BIU", 20, 40)))
         scan("SI", "KEEP", "GI")
+        tt("DA", "O", "E", sub)
+        tt(W("DB", 4, 16), W("E", 4, 16), W("O", 0, 12), sub)
         cp("SE", W("SI", 15, 256, 16))
         cp("SO", W("SI", 271, 512, 16))
         halfstep(0, False, [])
@@ -478,10 +492,22 @@ def rank_program(g, core, T, topo):
             act(W("HG", 128 * t, 128 * t + 128), I("PF%d" % t, aa))
         act("FX", I("FW", "SEL"))
         tt("FM", I("FW", "SEL"), "MASK", mul)
-        for t in range(4):
+
+        def arrived(t):
             tt(W("HT", t, 512, 4), I("PF%d" % t, ab), W("HG", 128 * t, 128 * t + 128), add)
+        arrived(0)
         scan("SCN", "KEEP", "FM")
+        arrived(1)
+        tt("EQB", "FX", "SCN", eq)
+        cp("FC", W("SCN", 15, 512, 16))
+        if rd + 1 < ROUNDS:
+            dmas("dc%d" % rd, [("y", W("TR", 0, 32, 1, 32 * Q, 32 * Q + 32), W("FC", 0, 32, 1, Q, 128, 4)) for Q in range(4)])
+        arrived(2)
+        scan("CNT", "KEEPB", "EQB")
+        arrived(3)
+        ts("LZ", W("CNT", 15, 512, 16), 1.5, gt, pf(0), mul)
         quant("aq", "asc", "HT")
+        tt("OF", "FC", "LZ", mx_)
         for b in range(4):
             mm(3 + b, "wq", "wsc", 128 * b, "aq", "asc")
             act(W("YW%d" % b, 0, 128), W("ps%d" % (3 + b), 0, 128), 2.0 ** -6)
@@ -489,15 +515,6 @@ def rank_program(g, core, T, topo):
             fr = I("FX", "REV")
             op("s", lambda: g.scalar.activation(ap("FXR"), ap(fr), ACT.Identity, bias=-float(BIAS)), [fr], ["FXR"])
             dmas("dad", [("y", T.ad[:, :], W("FXR", 0, 512, 1, 0, 128, 16))])
-        tt("EQB", "FX", "SCN", eq)
-        cp("FC", W("SCN", 15, 512, 16))
-        if rd + 1 < ROUNDS:
-            dmas("dc%d" % rd, [("y", W("TR", 0, 32, 1, 32 * Q, 32 * Q + 32), W("FC", 0, 32, 1, Q, 128, 4)) for Q in range(4)])
-        scan("CNT", "KEEPB", "EQB")
-        ts("N1", "FC", -1.0, mul, pf(0), add)
-        ts("LZ", W("CNT", 15, 512, 16), 1.5, gt)
-        tt("N2", "LZ", "N1", mul)
-        tt("OF", "FC", "N2", add)
         ts(W("OFF", 0, 32, 2), W("OF", 0, 32, 2), -float(BIAS), add)
         ts(W("OFF", 1, 32, 2), W("OF", 1, 32, 2), 336.0 - BIAS, add)
         for k in range(15, -1, -1):

from concourse.mybir import dt, AluOpType, AxisListType, ActivationFunctionType

ROUNDS = 3
FAR = 1e29
BIAS = 8
F32, BF, I32, U16, MXC, U8 = "float32", "bfloat16", "int32", "uint16", "float8_e4m3fn_x4", "uint8"
SCRATCH, PART = {}, {}


def _sb(dtype, **kw):
    for k, n in kw.items():
        SCRATCH[k] = ("sbuf", [128, n], dtype)
        PART[k] = (k, 0, n)


def _pack(buf, dtype, **kw):
    at = 0
    for k, n in kw.items():
        PART[k] = (buf, at, n)
        at += (n + 15) // 16 * 16
    SCRATCH[buf] = ("sbuf", [128, at], dtype)


_sb(BF, XT=1280, MT=1280, UT=512, VT=512, BY=512, ON=512, DT=512, HT=512, HG=512)
_pack("CTB", BF, CT0=512, CT1=512, CT2=512, CT3=512)
_pack("CBB", BF, CB0=512, CB7=512)
_pack("YW", BF, YW0=960, YW1=960, YW2=960, YW3=960)
_pack("FH", BF, FH0=320, FH1=320, FH2=320, FH3=320)
_pack("FQ", BF, FQ0=320, FQ1=320, FQ2=320, FQ3=320)
_pack("PF", BF, PF0=320, PF1=320, PF2=320, PF3=320)
_pack("ZG", BF, ZG0=512, ZG1=512, ZG2=512, ZG3=512)
_sb(MXC, uq=128, ur=1152, vq=128, dq=128, aq=128, wq=512, mq0=320, mq1=320, mq2=320, mq3=320, lq0=320, lq1=320, lq2=320)
_sb(U8, us=128, urs=1152, vs=128, dsc=128, asc=128, wsc=512, ms0=320, ms1=320, ms2=320, ms3=320, ls0=320, ls1=320, ls2=320)
_pack("eqc", MXC, eq0=128, eq1=128, eq2=128, eq3=128, bq0=128, bq7=128)
_pack("esc", U8, es0=128, es1=128, es2=128, es3=128, bs0=128, bs7=128)
_sb(F32, IOTA=4096, IO512=320, LOWC=672, PLC=512)
_pack("KC", F32, MASK=512, KEEP=512, ONES=320, JK=4, CE=32, CIDX=20, PCF=4, JKN=32, HN=32)
_sb(BF, KEEPB=512)
_sb(I32, CI=512, CJ=32, PCI=4)
_sb(F32, W07=320, ST=3200, NB8=2560, KT0=320, KT7=320, YO=320)
_pack("BN", F32, GB=320, M1=160, M2=80, M3=40, NE8=320, SC8=320)
_sb(I32, LBI=20, NBI=160, PI=32)
_sb(U16, LB=20, NBL=160, ULU=72)
SCRATCH["NBD"] = ("dram", [16, 160], I32)
_pack("HB", F32, RB=32, E=16, O=16, SE=16, SO=16, DA=16, DB=20, SM=16, PR=16, NV=16, SYV=16, SG1=16, KK=16, E4=4, SYE=4, KD=4, GTB=4, G2=4, SG2=4, GT=16, GD=16, R=36, NE=28, D4=4, KR=32, NK=4, TA=96, PS=4, PP=32, PT=32, PF32=32, ISL=32, PD=32, PM=32, SELF=32, FC=32, LZ=32, OF=32, BI=40, GK=64, SK=64, GB2=64, SB=64, GS=256, SS=256, GI=512, SI=512, G8=128, S8=128)
_sb(F32, TR=32, RK=512, SG=512, FW=640, DP=512, SRT=512, SELX=512, FM=512, SCN=512, FX=512, LOWA=672, LOWB=672, LO1=640, LO2=320, REVF=32, XE=320, XS=320, FXR=512)
_sb(BF, CMP=512, EQB=512, CNT=512)
_pack("HI", I32, P8=8, P8A=8, P8B=8, XI=20, XJ=20)
_pack("HU", U16, OFFI=32, KOU=4, KU=16, KU2=4, TU=96, PU=32, SEL=32, EL=20, OFF=32, REV=32, BIU=40)
_sb(U16, AL=96, PA=32, SL0=16, SL1=16, SL2=16, AR0=16, AR1=16, AR2=16)
for _t in range(8):
    SCRATCH["ps%d" % _t] = ("psum", [128, 512], F32)

SEMAPHORES = ["sv", "st", "ss", "sg", "dx", "du", "dv", "dw", "dp", "dlb", "dnb", "dnl", "rsend", "dad", "doc", "dy"]
for _t in range(3):
    SEMAPHORES += ["da%d" % _t, "db%d" % _t, "dc%d" % _t, "rq%d" % _t, "rl%d" % _t]


def rank_program(g, core, T, topo):
    rank = T.rank_of(core)
    if rank is None:
        return
    A, ACT = AluOpType, ActivationFunctionType
    add, sub, mul, mx_, mn_, eq, ne, gt, lt = A.add, A.subtract, A.mult, A.max, A.min, A.is_equal, A.not_equal, A.is_gt, A.is_lt
    bw, shr = A.bitwise_and, A.arith_shift_right
    queue = {"v": g.vector, "t": g.tensor, "s": g.scalar, "y": g.sync, "g": g}
    own = {"v": "sv", "t": "st", "s": "ss", "g": "sg"}
    count = {k: 0 for k in own}
    know = {k: {} for k in queue}
    hist, serial, totals = {}, [0], {}

    def W(name, a, b, st=1, p0=0, p1=128, ps=1):
        buf, at, _n = PART.get(name, (name, 0, 0))
        return (buf, a + at, b + at, st, p0, p1, ps)

    def N(v):
        return W(v, 0, PART[v][2]) if isinstance(v, str) else v

    def I(win, off):
        return ("I", N(win), N(off))

    def ap(v):
        v = N(v)
        if v[0] == "I":
            return ap(v[1]).indirect(ap(v[2]))
        n, a, b, st, p0, p1, ps = v
        rows = slice(p0, p1, ps) if ps != 1 else slice(p0, p1)
        cs = slice(a, b, st) if st != 1 else slice(a, b)
        return T[n][rows, cs]

    def meet(a, b, s, c, d, u):
        if b <= c or d <= a:
            return False
        return not (s == u and s > 1 and (a - c) % s)

    def overlap(x, y):
        return meet(x[1], x[2], x[3], y[1], y[2], y[3]) and meet(x[4], x[5], x[6], y[4], y[5], y[6])

    def covers(x, y):
        return x[3] == 1 and x[6] == 1 and x[1] <= y[1] and x[2] >= y[2] and x[4] <= y[4] and x[5] >= y[5]

    def sync_for(q, reads, writes):
        todo = {}
        for v, w in [(v, False) for v in reads] + [(v, True) for v in writes]:
            bank = v[0].startswith("ps")
            for h in hist.get(v[0], ()):
                if not (w or h["w"] or (bank and h["q"] != q)):
                    continue
                if not bank and not overlap(v, h["v"]):
                    continue
                if know[q].get(h["sem"], 0) < h["val"]:
                    if h["sem"] not in todo or todo[h["sem"]]["val"] < h["val"]:
                        todo[h["sem"]] = h
        for h in sorted(todo.values(), key=lambda h: -h["n"]):
            if know[q].get(h["sem"], 0) >= h["val"]:
                continue
            queue[q].wait_ge(T.sem[h["sem"]], h["val"])
            for s, x in h["snap"].items():
                know[q][s] = max(know[q].get(s, 0), x)
            know[q][h["sem"]] = h["val"]

    def note(q, reads, writes, sem, val, late, snap=None):
        serial[0] += 1
        snap = dict(know[q]) if snap is None else snap
        for v, w in [(v, False) for v in reads] + [(v, True) for v in writes]:
            old = hist.setdefault(v[0], [])
            if w:
                old[:] = [h for h in old if not covers(v, h["v"])]
            else:
                old[:] = [h for h in old if not (not h["w"] and h["q"] == q and not late and not h["late"] and h["v"] == v)]
            old.append({"v": v, "w": w, "q": q, "late": late, "sem": sem, "val": val, "snap": snap, "n": serial[0]})

    def op(q, call, reads, writes):
        rd, wr = [], []
        for v in map(N, reads):
            rd += [v[1], v[2]] if v[0] == "I" else [v]
        for v in map(N, writes):
            wr.append(v[1] if v[0] == "I" else v)
            rd += [v[2]] if v[0] == "I" else []
        sync_for(q, rd, wr)
        if q == "g" and know[q].get("sg", 0) < count[q]:
            g.wait_ge(T.sem["sg"], count[q])
            know[q]["sg"] = count[q]
        count[q] += 1
        call().then_inc(T.sem[own[q]], 1)
        note(q, rd, wr, own[q], count[q], False)

    def cp(out, a):
        op("v", lambda: g.vector.tensor_copy(ap(out), ap(a)), [a], [out])

    def tt(out, a, b, o):
        op("v", lambda: g.vector.tensor_tensor(ap(out), ap(a), ap(b), o), [a, b], [out])

    def ts(out, a, s1, o0, s2=None, o1=None):
        x1, x2 = [ap(s) if isinstance(s, tuple) else s for s in (s1, s2)]
        more = () if o1 is None else (o1,)
        op("v", lambda: g.vector.tensor_scalar(ap(out), ap(a), x1, x2, o0, *more), [a] + [s for s in (s1, s2) if isinstance(s, tuple)], [out])

    def scan(out, d0, d1):
        op("v", lambda: g.vector.tensor_tensor_scan(ap(out), ap(d0), ap(d1), 0.0, mul, add), [d0, d1], [out])

    def red(out, a):
        op("v", lambda: g.vector.tensor_reduce(ap(out), ap(a), AxisListType.X, add), [a], [out])

    def fill(out, c):
        op("v", lambda: g.vector.memset(ap(out), c), [], [out])

    def tr(out, a):
        op("v", lambda: g.vector.transpose(ap(out), ap(a)), [a], [out])

    def quant(q, s, a):
        op("v", lambda: g.vector.quantize_mx(ap(q), ap(s), ap(a)), [a], [q, s])

    def act(out, a, scale=1.0):
        more = {} if scale == 1.0 else {"scale": scale}
        op("s", lambda: g.scalar.activation(ap(out), ap(a), ACT.Copy, **more), [a], [out])

    def iota(out, pattern, base, mult):
        more = {"allow_small_or_imprecise_dtypes": True} if SCRATCH[N(out)[0]][2] == F32 else {}
        op("g", lambda: g.iota(ap(out), pattern, base, mult, **more), [], [out])

    def select(out, a, pattern, base, mult):
        op("g", lambda: g.affine_select(ap(out), ap(a), pattern, eq, 0.0, base, mult), [a], [out])

    def mm(bank, lq, ls, l0, rq, rs):
        a, b, o = W(lq, l0, l0 + 128), W(ls, l0, l0 + 128), W("ps%d" % bank, 0, PART[rq][2])
        op("t", lambda: g.tensor.matmul_mx(ap(o), ap(a), ap(b), ap(rq), ap(rs), True, True), [a, b, rq, rs], [o])

    def dmas(sem, items):
        done, total = [], 16 * len(items)
        totals[sem] = total

        def side(v):
            if isinstance(v, tuple) and v[0] == "C":
                return ap(v[1]).bitcast(dt.uint8), [N(v[1])]
            return (ap(v), [N(v)]) if isinstance(v, (tuple, str)) else (v, [])
        for q, out, a in items:
            (o, ow), (i, ir) = side(out), side(a)
            sync_for(q, ir, ow)
            queue[q].dma_start(o, i).then_inc(T.sem[sem], 16)
            done.append((q, ir, ow, dict(know[q])))
        for q, ir, ow, snap in done:
            note(q, ir, ow, sem, total, True, snap)

    nxt, prv = T.cores[(rank + 1) % len(T.cores)], T.cores[(rank - 1) % len(T.cores)]
    a_nxt, m_nxt = topo.addr(nxt), topo.mask(core, nxt)
    e_out, e_in = len(topo.engines(core, nxt)), len(topo.engines(prv, core))
    sent = [0]

    def send(out, src, rsem, code=False):
        sync_for("g", [N(src)], [])
        o, i = ap(out), ap(src)
        if code:
            o, i = o.bitcast(dt.uint8), i.bitcast(dt.uint8)
        g.remote_dma(o, i, T.sem[rsem], T.sem["rsend"], a_nxt[1], a_nxt[0], m_nxt)
        sent[0] += e_out

    def arrival(names, sem, n):
        totals[sem] = n
        note("r", [], [N(v) for v in names], sem, n, True, {})

    dmas("dx", [("y", "XT", T.x[:, :])])
    dmas("du", [("s", "UT", T.u[:, :])])
    dmas("dlb", [("ys"[t % 2], W("LBI", 0, 20, 1, 8 * y + 7 - t, 128, 16), T.nb[16 * t + 8 * y:16 * t + 8 * y + 8, :]) for y in range(2) for t in range(8)])
    dmas("dp", [("ys"[(b + Q) % 2], W("PI", 0, 32, 1, 32 * Q + b, 32 * Q + 32, 4), T.p[15 - 4 * b - Q:128:16, :]) for Q in range(4) for b in range(4)])
    dmas("dnb", [("ys"[k % 2], W("NBD", 20 * k, 20 * k + 20, 1, 8 * y, 8 * y + 8), T.nb[2 * k + y:128:16, :]) for k in range(8) for y in range(2)])
    dmas("dnl", [("y", W("NBI", 0, 160, 1, 16 * k, 16 * k + 16), W("NBD", 0, 160, 1, 0, 16)) for k in range(8)])
    dmas("dw", [("y", ("C", "wq"), T.wc[:, :]), ("y", "wsc", T.ws[:, :])])
    dmas("dv", [("y", "VT", T.v[:, :])])

    fill("BY", 0.0)
    for k in range(8):
        for y in range(2):
            fill(W("BY", 64 * k + 33 * y, 64 * k + 32 * y + 32, 4), 1.0)
    fill("ULU", 0)
    fill("DT", 0.0)
    iota(W("PCI", 0, 1), [[0, 1]], 0, 1)
    iota(W("IOTA", 0, 320), [[1, 320]], 0, 0)
    for e in (0, 7):
        select("CB%d" % e, "BY", [[0, 16], [-16, 8], [0, 4]], 0 if e == 0 else -8, 1)
    iota("CI", [[0, 32], [-1, 16]], 16, 1)
    iota("CIDX", [[16, 20]], -1, 0)
    for Q in range(4):
        iota(W("JK", 0, 4, 1, 32 * Q, 32 * Q + 32), [[-4, 4]], 7 * 512 + 15 - Q, 16)
    iota("CE", [[16, 32]], 128, 0)
    iota("CJ", [[16, 32]], 15, 0)

    def later_constants():
        for b in range(4):
            select("CT%d" % b, "ON", [[1, 512]], -b, -4)
        iota(W("LOWC", 0, 336), [[1, 336]], 512 * 1024 + 640, 0)
        iota(W("LOWC", 336, 672), [[1, 336]], 512 * 1024 + 640, 0)
        iota("PLC", [[16384, 32], [-1024, 16]], 15 * 1024, 0)
        iota("IO512", [[512, 320]], 0, 0)
        iota(W("IOTA", 320, 4096), [[1, 3776]], 320, 0)

    pc, pf = (lambda i: W("PCI", i, i + 1)), (lambda i: W("PCF", i, i + 1))
    ts(pc(1), pc(0), 15, bw)
    ts(pc(2), pc(0), 3, shr, 1, bw)
    cp(pf(0), pc(1))
    cp(pf(1), pc(2))
    ts(W("ULU", 0, 8), W("ULU", 8, 16), pf(1), add, 112.0, mul)
    for k in range(1, 8):
        fill(W("ULU", 8 + 8 * k, 16 + 8 * k), 16 * k)
    quant("uq", "us", "UT")

    def pick_u(a, b):
        ul, o = W("ULU", a // 16, b // 16), W("ur", a, b)
        op("v", lambda: g.vector.tensor_copy(ap(o).bitcast(dt.uint32), ap("uq").bitcast(dt.uint32).indirect(ap(ul))), ["uq", ul], [o])
        act(W("urs", a, b), I("us", ul))
    pick_u(0, 128)
    quant("mq0", "ms0", "XT")
    pick_u(128, 1152)
    for e in (0, 7):
        quant("bq%d" % e, "bs%d" % e, "CB%d" % e)
    fill("ONES", 1.0)
    fill("ON", 1.0)
    cp("LB", "LBI")
    ts("TR", "PI", float(BIAS), add)
    CELLS, CELLS8 = W("IOTA", 0, 320), W("IOTA", BIAS, BIAS + 320)

    def more_constants():
        cp("NBL", "NBI")
        act(W("NB8", 0, 1600), I(CELLS, W("NBL", 0, 100)))
        for k in ("KEEP", "KEEPB"):
            fill(k, 1.0)
        ts("CI", "CI", 15, bw)
        for k in ("KEEP", "KEEPB"):
            fill(W(k, 0, 512, 16), 0.0)
        ts("MASK", "CI", 0.0, eq)
        ts("CE", "CE", pf(0), add)
        ts(pc(2), pc(1), 1, shr)
        ts(pc(3), pc(1), 1, bw)
        fill("DB", 0.0)
        ts(pf(2), pc(2), 320.0, mul)
        ts(pf(3), pc(3), 8.0, mul)
        for k in (0, 2880):
            fill(W("ST", k, k + 320), 0.0)
        ts("CIDX", "CIDX", pf(2), add, pf(3), add)
        ts(pf(0), pf(0), 320.0 + BIAS, add)
        cp(W("NB8", 1600, 2560), I(CELLS, W("NBL", 100, 160)))

    def last_constants():
        for b in range(4):
            quant("eq%d" % b, "es%d" % b, "CT%d" % b)
        for k in range(8):
            ts(W("JKN", 4 * k, 4 * k + 4), "JK", -1.0 / 512, mul)
        fill("HN", -511.0)
        fill(W("HN", 3, 32, 4), 0.0)

    def end_constants():
        quant("vq", "vs", "VT")
        ts("REVF", "CJ", pf(0), sub, 320.0 + BIAS, add)
        cp("REV", "REVF")

    MASK, KEEP = (lambda n: W("MASK", 0, n)), (lambda n: W("KEEP", 0, n))

    def halfstep(par, last, fillers):
        Y, S, oth = ("E", "SE", "O") if par == 0 else ("O", "SO", "E")
        eb, i0, ge, kt = (0, 4, 0, "KT0") if par == 0 else (12, 0, 7, "KT7")
        e = lambda n: W(n, eb, eb + 4)
        m, dbv, off = e(oth), (W("DB", 0, 16) if par == 0 else W("DB", 4, 20)), 320.0 * (ge + 1)
        cp("KOU", m)
        ts(e("KU"), m, off, add)
        if par == 0:
            tt(W("KK", 4, 16), W("O", 4, 16), W("DB", 4, 16), sub)
        else:
            tt(W("KK", 0, 12), W("E", 4, 16), W("DA", 0, 12), sub)
        tt("PR", "DA", dbv, mul)
        ts("E4", e("DA"), 0.0, ne, FAR, mul)
        tt("GK", I(kt, "KOU"), MASK(64), mul)
        for i in range(i0 // 4, i0 // 4 + 3):
            ts(W("KU", 4 * i, 4 * i + 4), W("KK", 4 * i, 4 * i + 4), 320.0 * (2 * i + par + 1), add)
        ts("NV", "PR", 0.0, ne, FAR, mul)
        tt("SYE", e(S), "E4", add)
        scan("SK", KEEP(64), "GK")
        tt("GS", I("ST", "KU"), MASK(256), mul)
        tt("SM", *(("DA", dbv) if par == 0 else (dbv, "DA")), sub)
        tt("SYV", S, "NV", add)
        for f in fillers:
            f()
        k0, sk, sb = W("SK", 15, 64, 16), W("SS", 15, 256, 16), W("SB", 15, 64, 16)
        ts("KU2", k0, off, add)
        scan("SS", KEEP(256), "GS")
        tt("KD", k0, m, sub)
        tt("GB2", I("ST", "KU2"), MASK(64), mul)
        tt("GT", sk, "SYV", gt)
        scan("SB", KEEP(64), "GB2")
        tt("GD", "GT", "SM", mul)
        tt("GTB", sb, "SYE", gt)
        if last and par == 1:
            for i in (3, 0, 1, 2):
                tt(W("R", 8 * i + 4, 8 * i + 8), W("O", 4 * i, 4 * i + 4), W("GD", 4 * i, 4 * i + 4), add)
        else:
            tt(Y, Y, "GD", add)
            tt("DA", "DA", "GD", sub if par == 0 else add)
            if par == 0:
                tt(W("DB", 4, 16), W("DB", 4, 16), W("GD", 4, 16), add)
            else:
                tt(W("DB", 4, 16), W("DB", 4, 16), W("GD", 0, 12), sub)
        tt("G2", "GTB", "KD", mul)
        if not last:
            tt("SG1", sk, "NV", sub)
            tt("SG2", sb, "E4", sub)
            tt(S, S, "SG1", mx_)
        if last and par == 1:
            tt(W("R", 28, 32), W("R", 28, 32), "G2", add)
        else:
            tt(e("DA"), e("DA"), "G2", sub if par == 0 else add)
            tt(e(Y), e(Y), "G2", add)
        if not last:
            tt(e(S), e(S), "SG2", mx_)

    for rd in range(ROUNDS):
        mq, ms, lq, ls, sl, ar = "mq%d" % rd, "ms%d" % rd, "lq%d" % rd, "ls%d" % rd, "SL%d" % rd, "AR%d" % rd
        send(lq, mq, "rq%d" % rd, True)
        send(ls, ms, "rq%d" % rd)
        arrival([lq, ls], "rq%d" % rd, 2 * e_in)
        if rd == 0:
            later_constants()
        mm(0, "ur", "urs", 0, mq, ms)
        for k in range(8):
            mm((k + 1) % 8, "ur", "urs", 128 + 128 * k, mq, ms)
            if k == 0:
                act("W07", W("ps0", 0, 320))
            act(W("ST", 320 * k + 320, 320 * k + 640), W("ps%d" % ((k + 1) % 8), 0, 320))
        tr("RB", "TR")
        for i in range(4):
            for par in range(2):
                src = W("RB", 8 * i + 4 * par, 8 * i + 4 * par + 4)
                ts(W("OFFI", 16 * par + 4 * i, 16 * par + 4 * i + 4), src, 320.0 * (2 * i + par + 1) - BIAS, add)
                ts(W("EO"[par], 4 * i, 4 * i + 4), src, -float(BIAS), add)
        cp("GB", I("W07", "LB"))
        tt("M1", W("GB", 0, 320, 2), W("GB", 1, 320, 2), mx_)
        tt("M2", W("M1", 0, 160, 2), W("M1", 1, 160, 2), mx_)
        tt("M3", W("M2", 0, 80, 2), W("M2", 1, 80, 2), mx_)
        for t in range(8):
            tt(W("NE8", t, 320, 8), W("GB", t, 320, 8), "M3", ne)
        scan("SC8", "NE8", "ONES")
        cp(W("DT", 0, 80, 4), W("SC8", 7, 320, 16))
        cp(W("DT", 1, 80, 4), W("SC8", 15, 320, 16))
        quant("dq", "dsc", "DT")
        mm(1, "bq0", "bs0", 0, "dq", "dsc")
        mm(2, "bq7", "bs7", 0, "dq", "dsc")
        if rd == 0:
            more_constants()
        tt("GI", I("ST", "OFFI"), "MASK", mul)
        tt(W("BI", 0, 20), W("ps1", 0, 20), "CIDX", add)
        tt(W("BI", 20, 40), W("ps2", 0, 20), "CIDX", add)
        cp("BIU", "BI")
        act("KT0", I("NB8", W("BIU", 0, 20)))
        act("KT7", I("NB8", W("BIU", 20, 40)))
        scan("SI", "KEEP", "GI")
        tt("DA", "O", "E", sub)
        tt(W("DB", 4, 16), W("E", 4, 16), W("O", 0, 12), sub)
        cp("SE", W("SI", 15, 256, 16))
        cp("SO", W("SI", 271, 512, 16))
        halfstep(0, False, [])
        if rd == 0:
            last_constants()
        for t in range(4):
            f = W("ps%d" % (3 + t), 0, 320)
            mm(3 + t, "eq%d" % t, "es%d" % t, 0, mq, ms)
            act("FQ%d" % t, f, 0.25)
            act("FH%d" % t, f, 0.5)
            act(W("YW%d" % t, 640, 960), f, 0.5)
        act("LOWA", "LOWC")
        act("LOWB", "LOWC")
        for t in range(4):
            k = (7, 0, 1, 2)[t]
            mm(k, "eq%d" % t, "es%d" % t, 0, lq, ls)
            act("PF%d" % t, W("ps%d" % k, 0, 320), 0.5)
        halfstep(1, False, [])
        halfstep(0, True, [])
        halfstep(1, True, [lambda i=i: cp(W("R", 8 * i, 8 * i + 4), W("E", 4 * i, 4 * i + 4)) for i in range(4)] + [lambda: cp(W("R", 32, 36), W("E", 12, 16))])
        tt("NE", W("R", 0, 28), W("R", 4, 32), ne)
        tr(W("TA", 0, 32), W("R", 0, 32))
        tr(W("TA", 32, 64), W("R", 4, 36))
        for b in range(4):
            red(W("D4", b, b + 1), W("NE", b, 28, 4))
        for b in range(4):
            ts(W("KR", b, 32, 4), W("JKN", b, 32, 4), W("D4", b, b + 1), add, -512.0, mul)
        tr(W("TA", 64, 96), "KR")
        ts("NK", W("KR", 0, 4), -1.0, mul)
        cp("TU", "TA")
        dmas("da%d" % rd, [("ys"[Q % 2], W("AL", 0, 96, 1, Q, 128, 4), W("TU", 0, 96, 1, 32 * Q, 32 * Q + 32)) for Q in range(4)])
        if rd == 0:
            end_constants()
        al, bl, kl = W("AL", 0, 32), W("AL", 32, 64), W("AL", 64, 96)
        cp("RK", I("IOTA", kl))
        for b in range(3):
            bi, ac = W("NK", b, b + 1), W("PS", b, b + 1)
            op("s", lambda: g.scalar.activation(ap("SG"), ap("RK"), ACT.Sign, bias=ap(bi), accum_out=ap(ac)), ["RK", bi], ["SG", ac])
        act(W("FW", 128, 640), I(CELLS8, al))
        ts("CMP", "RK", W("KR", 3, 4), lt, -2.0, mul)
        red(W("PS", 3, 4), "CMP")
        for b in range(4):
            ts(W("PP", b, 32, 4), W("HN", b, 32, 4), W("PS", b, b + 1), add, -0.5, mul)
        tr("PT", "PP")
        cp("PU", "PT")
        dmas("db%d" % rd, [("y", W("PA", 0, 32, 1, Q, 128, 4), W("PU", 0, 32, 1, 32 * Q, 32 * Q + 32)) for Q in range(4)])
        tt("DP", I("IO512", bl), W("FW", 128, 640), add)
        for t in range(4):
            act("ZG%d" % t, I("FQ%d" % t, al))

        def bonds(t):
            tt(W("YW%d" % t, 128, 640), I("FQ%d" % t, bl), "ZG%d" % t, add)
        bonds(0)
        bonds(1)
        cp(I("SRT", "PA"), "DP")
        cp("PF32", "PA")
        tt("G8", W("SRT", 0, 128), MASK(128), mul)
        ts("ISL", "PF32", 128.0, lt)
        scan("S8", KEEP(128), "G8")
        tt("PD", "PF32", "CE", sub)
        cp("P8", W("S8", 15, 128, 16))
        tt("PM", "PD", "ISL", mul)
        ts("P8A", "P8", 511, bw)
        ts("P8B", "P8", 9, shr)
        tt("SELF", "PM", "CE", add)
        ts(W(sl, 0, 8), "P8A", -float(BIAS), add)
        cp(W(sl, 8, 16), "P8B")
        cp("SEL", "SELF")
        send(ar, sl, "rl%d" % rd)
        arrival([ar], "rl%d" % rd, e_in)
        tt("SELX", I("IOTA", "SEL"), "PLC", add)
        bonds(2)
        bonds(3)
        aa, ab = W(ar, 0, 8), W(ar, 8, 16)
        cp(W("FW", 0, 128), I(CELLS8, aa))
        for t in range(4):
            act(W("HG", 128 * t, 128 * t + 128), I("PF%d" % t, aa))
        act("FX", I("FW", "SEL"))
        tt("FM", I("FW", "SEL"), "MASK", mul)

        def arrived(t):
            tt(W("HT", t, 512, 4), I("PF%d" % t, ab), W("HG", 128 * t, 128 * t + 128), add)
        arrived(0)
        scan("SCN", "KEEP", "FM")
        arrived(1)
        tt("EQB", "FX", "SCN", eq)
        cp("FC", W("SCN", 15, 512, 16))
        if rd + 1 < ROUNDS:
            dmas("dc%d" % rd, [("y", W("TR", 0, 32, 1, 32 * Q, 32 * Q + 32), W("FC", 0, 32, 1, Q, 128, 4)) for Q in range(4)])
        arrived(2)
        scan("CNT", "KEEPB", "EQB")
        arrived(3)
        ts("LZ", W("CNT", 15, 512, 16), 1.5, gt, pf(0), mul)
        quant("aq", "asc", "HT")
        tt("OF", "FC", "LZ", mx_)
        for b in range(4):
            mm(3 + b, "wq", "wsc", 128 * b, "aq", "asc")
            act(W("YW%d" % b, 0, 128), W("ps%d" % (3 + b), 0, 128), 2.0 ** -6)
        if rd + 1 == ROUNDS:
            fr = I("FX", "REV")
            op("s", lambda: g.scalar.activation(ap("FXR"), ap(fr), ACT.Identity, bias=-float(BIAS)), [fr], ["FXR"])
            dmas("dad", [("y", T.ad[:, :], W("FXR", 0, 512, 1, 0, 128, 16))])
        ts(W("OFF", 0, 32, 2), W("OF", 0, 32, 2), -float(BIAS), add)
        ts(W("OFF", 1, 32, 2), W("OF", 1, 32, 2), 336.0 - BIAS, add)
        for k in range(15, -1, -1):
            cp(I("LOWA" if k % 2 else "LOWB", W("OFF", 2 * k, 2 * k + 2)), W("SELX", 32 * k, 32 * k + 32))
        for i in range(2):
            tt(W("LO1", 320 * i, 320 * i + 320), W("LOWA", 336 * i, 336 * i + 320), W("LOWB", 336 * i, 336 * i + 320), mn_)
        tt("LO2", W("LO1", 0, 320), W("LO1", 320, 640), mn_)
        tt("XE", "LO2", MASK(320), mul)
        scan("XS", KEEP(320), "XE")
        cp("XI", W("XS", 15, 320, 16))
        ts("XJ", "XI", 1023, bw)
        cp("EL", "XJ")
        for t in range(4):
            tt(W("MT", t, 1280, 4), I("YW%d" % t, "EL"), "FH%d" % t, add)
        quant("mq%d" % (rd + 1), "ms%d" % (rd + 1), "MT")

    mq, ms = "mq%d" % ROUNDS, "ms%d" % ROUNDS
    mm(0, "vq", "vs", 0, mq, ms)
    act("YO", W("ps0", 0, 320))
    dmas("doc", [("y", T.oc[:, :], ("C", mq))] + [("y", T.osc[4 * k:4 * k + 4, :], W(ms, 0, 320, 1, 32 * k, 32 * k + 4)) for k in range(4)])
    dmas("dy", [("s", T.y[:, :], "YO")])

    g.wait_ge(T.sem["rsend"], sent[0])
    for q in own:
        g.wait_ge(T.sem[own[q]], count[q])
    for s in sorted(totals):
        g.wait_ge(T.sem[s], totals[s])
